import numpy as np
import ml_dtypes


def mxq(x, axis, fmt="e4m3"):
    dtype, down = {"e4m3": (ml_dtypes.float8_e4m3fn, 7), "e5m2": (ml_dtypes.float8_e5m2, 14)}[fmt]
    v = np.moveaxis(np.asarray(x, np.float32).astype(ml_dtypes.bfloat16).astype(np.float64), axis, -1)
    blocks = v.reshape(v.shape[:-1] + (-1, 32))
    amax = np.abs(blocks).max(-1, keepdims=True)
    byte = np.maximum(np.where(amax > 0, np.frexp(amax)[1] - 1 + 127, 0) - down, 1)
    scale = np.exp2(byte - 127.0)
    codes = (blocks / scale).astype(np.float32).astype(dtype).astype(np.float64)
    return np.moveaxis((codes * scale).reshape(v.shape), -1, axis)


WIDE = False


def mx_kscale(k):
    if not WIDE:
        return np.ones(k)
    levels = np.array([10, -10, 5, -5, 0])
    if k % 512:
        return np.exp2(np.random.permutation(np.resize(levels, k // 32))).repeat(32)
    a = np.empty((k // 512, 16))
    for p in range(k // 512):
        a[p, :8] = np.random.permutation(np.resize(levels, 8))
        for g in range(8):
            far = levels[np.abs(levels - a[p, g]) >= 10]
            a[p, g + 8] = far[np.random.randint(len(far))]
    return np.exp2(a.ravel()).repeat(32)


def f64(x):
    return np.asarray(x).astype(np.float64)


def striped(idx):
    return np.tile(idx.reshape(-1, 16).T, (8, 1)).astype(np.uint16)


def unstriped(offs):
    return offs[:16].T.reshape(-1).astype(np.int64)


def pack_weight(w):
    k, n = w.shape
    w = f64(np.asarray(w, np.float32).astype(ml_dtypes.bfloat16)).reshape(k // 32, 32, n)
    amax = np.abs(w).max(1)
    byte = np.clip(np.where(amax > 0, np.frexp(amax)[1] - 1 + 127 - 7, 1), 1, 254)
    scaled = (w * np.exp2(127.0 - byte)[:, None, :]).reshape(k, n).astype(np.float32)
    words = np.ascontiguousarray(scaled.reshape(k // 512, 128, 4, n).transpose(0, 1, 3, 2)).astype(ml_dtypes.float8_e4m3fn).view(np.uint8)
    return words, np.ascontiguousarray(byte.astype(np.uint8).reshape(k // 512, 16, n))


def unpack_weight(words, scales):
    g, p, n, _ = words.shape
    vals = np.ascontiguousarray(words).view(ml_dtypes.float8_e4m3fn).astype(np.float64) * np.repeat(np.exp2(scales.astype(np.float64) - 127.0), 8, axis=1)[..., None]
    return vals.transpose(0, 1, 3, 2).reshape(g * 512, n)


E2M1 = np.array([0.0, 0.5, 1.0, 1.5, 2.0, 3.0, 4.0, 6.0, -0.0, -0.5, -1.0, -1.5, -2.0, -3.0, -4.0, -6.0])


def pack_fp4(w):
    k, n = w.shape
    w = f64(np.asarray(w, np.float32).astype(ml_dtypes.bfloat16)).reshape(k // 32, 32, n)
    amax = np.abs(w).max(1)
    mant, ex = np.frexp(amax / 6.0)
    byte = np.clip(np.where(amax > 0, np.where(mant > 0.5, ex, ex - 1) + 127, 1), 1, 254)
    scaled = (w * np.exp2(127.0 - byte)[:, None, :]).reshape(k, n).astype(np.float32)
    c = np.ascontiguousarray(scaled.reshape(k // 512, 128, 4, n).transpose(0, 1, 3, 2)).astype(ml_dtypes.float4_e2m1fn).view(np.uint8) & 0xF
    words = (c[..., 0::2] | (c[..., 1::2] << 4)).reshape(k // 512, 128, 2 * n)
    return np.ascontiguousarray(words), np.ascontiguousarray(byte.astype(np.uint8).reshape(k // 512, 16, n))


def unpack_fp4(words, scales):
    g, _, n = scales.shape
    words = np.ascontiguousarray(words).reshape(g, 128, n, 2)
    nib = np.empty((g, 128, n, 4), np.uint8)
    nib[..., 0::2] = words & 0xF
    nib[..., 1::2] = words >> 4
    vals = E2M1[nib] * np.repeat(np.exp2(scales.astype(np.float64) - 127.0), 8, axis=1)[..., None]
    return vals.transpose(0, 1, 3, 2).reshape(g * 512, n)


def gelu(v):
    return 0.5 * v * (1.0 + np.tanh(np.sqrt(2.0 / np.pi) * (v + 0.044715 * v**3)))


K, T, S, H, N = 512, 2048, 1024, 512, 256


def setup_inputs():
    n = np.random.standard_normal
    s = mx_kscale(K)[:, None]
    u = mx_kscale(H)
    packed_xT = pack_weight(n((K, T)) * s)
    packed_w2 = pack_fp4(n((H, N)) / np.sqrt(H) / u[:, None])
    return {
        "x_words": packed_xT[0],
        "x_scales": packed_xT[1],
        "w1": (n((K, H)) / np.sqrt(K) / s * u).astype(np.float32),
        "w2_words": packed_w2[0],
        "w2_scales": packed_w2[1],
        "pos": (0.5 * n((H, S)) * u[:, None]).astype(np.float32),
        "offs": striped(np.random.permutation(T)[(T * np.random.uniform(0, 1, S) ** 4).astype(np.int64)]),
    }


def reference(x_words, x_scales, w1, w2_words, w2_scales, pos, offs):
    xq = unpack_weight(x_words, x_scales)[:, unstriped(offs)]
    h = gelu((mxq(f64(w1), 0, "e4m3").T @ xq) + f64(pos))
    return unpack_fp4(w2_words, w2_scales).T @ mxq(h, 0, "e4m3")

@@ -1,0 +1,143 @@
+from contextlib import ExitStack
+
+import concourse.mybir as mybir
+
+K, T, S, H, N = 512, 2048, 1024, 512, 256
+FLOPS = 2 * K * H * S + 2 * H * N * S
+
+F32 = mybir.dt.float32
+BF16 = mybir.dt.bfloat16
+I32 = mybir.dt.int32
+U32 = mybir.dt.uint32
+U16 = mybir.dt.uint16
+U8 = mybir.dt.uint8
+FP8X4 = mybir.dt.float8_e4m3fn_x4
+FP4X4 = mybir.dt.float4_e2m1fn_x4
+GELU = mybir.ActivationFunctionType.Gelu_apprx_tanh
+ADD = mybir.AluOpType.add
+
+P = 128
+PACK = 4
+CHUNK = 256
+UNIT = 128
+VECTOR_COPIES = 1
+
+
+def tile_picked_embpos_gelu_p_kernel(tc, x_words, x_scales, w1, w2_words, w2_scales, pos, offs, out):
+    nc = tc.nc
+    with ExitStack() as ctx:
+        held = ctx.enter_context(tc.tile_pool(name="held", bufs=1))
+        work = ctx.enter_context(tc.tile_pool(name="work", bufs=4))
+        psum1 = ctx.enter_context(tc.psum_pool(name="psum1", bufs=5))
+        psum2 = ctx.enter_context(tc.psum_pool(name="psum2", bufs=3))
+
+        w1_rows = w1.rearrange("(p j) c -> p j c", j=PACK)
+        w1_raw = [held.tile([P, PACK, H // 2], F32, name="w1_raw%d" % half) for half in range(2)]
+        nc.sync.dma_start(w1_raw[0][:], w1_rows[:, :, : H // 2])
+
+        offsets = held.tile([P, S // 16], U16, name="offsets")
+        nc.sync.dma_start(offsets[:], offs)
+
+        scale_table = held.tile([P, T], U8, name="scale_table", align_bytes=64)
+        nc.vector.memset(scale_table[:].bitcast(I32), 0)
+        for q in range(4):
+            nc.sync.dma_start(scale_table[32 * q : 32 * q + 4, :].bitcast(I32), x_scales[0, 4 * q : 4 * q + 4, :].bitcast(I32))
+
+        warm_in = held.tile([P, 8], F32, name="warm_in")
+        warm_out = held.tile([P, 8], F32, name="warm_out")
+        nc.vector.memset(warm_in[:], 0.0)
+        nc.scalar.activation(warm_out[:], warm_in[:], GELU)
+
+        nc.sync.dma_start(w1_raw[1][:], w1_rows[:, :, H // 2 :])
+
+        word_table = held.tile([P, T], U32, name="word_table", align_bytes=64)
+        nc.sync.dma_start(word_table[:].bitcast(I32), x_words[0].rearrange("p n r -> p (n r)").bitcast(I32))
+
+        pos_rows = pos.rearrange("(p t) n -> p t n", t=PACK)
+        pos_chunks = []
+        w2_codes = held.tile([P, 2 * N], U8, name="w2_codes", align_bytes=64)
+        w2_plane = held.tile([P, N], U8, name="w2_plane", align_bytes=64)
+        nc.vector.memset(w2_plane[:].bitcast(I32), 0)
+        for c in range(S // CHUNK):
+            pos_chunk = held.tile([P, PACK, CHUNK], F32, name="pos_chunk%d" % c, tag="slot%d" % c, align_bytes=64)
+            nc.sync.dma_start(pos_chunk[:], pos_rows[:, :, c * CHUNK : (c + 1) * CHUNK])
+            pos_chunks.append(pos_chunk)
+            if c == 0:
+                nc.sync.dma_start(w2_codes[:].bitcast(I32), w2_words[0].bitcast(I32))
+                for q in range(4):
+                    nc.sync.dma_start(w2_plane[32 * q : 32 * q + 4, :].bitcast(I32), w2_scales[0, 4 * q : 4 * q + 4, :].bitcast(I32))
+
+        x_plane = held.tile([P, S], U8, name="x_plane", align_bytes=64)
+        nc.vector.tensor_copy(x_plane[:], scale_table[:].indirect(offsets[:]))
+
+        w1_grouped = held.tile([P, PACK, P, PACK], BF16, name="w1_grouped", align_bytes=64)
+        for half in range(2):
+            nc.scalar.copy(
+                w1_grouped[:, :, half * P // 2 : (half + 1) * P // 2, :].rearrange("p t m j -> p m j t"),
+                w1_raw[half][:].rearrange("p j (m t) -> p m j t", t=PACK),
+            )
+        w1_codes = held.tile([P, H], U32, name="w1_codes", align_bytes=64)
+        w1_plane = held.tile([P, H], U8, name="w1_plane", align_bytes=64)
+        nc.vector.quantize_mx(out=w1_codes[:].bitcast(FP8X4), scales=w1_plane[:], in_=w1_grouped[:].rearrange("p t m j -> p (t m j)"))
+
+        def gather_words(c):
+            tag = "x_codes%d" % c if c < 2 else "slot%d" % (c - 2)
+            codes = held.tile([P, CHUNK], U32, name="x_codes%d" % c, tag=tag, align_bytes=64)
+            nc.vector.tensor_copy(codes[:], word_table[:].indirect(offsets[:, c * CHUNK // 16 : (c + 1) * CHUNK // 16]))
+            return codes
+
+        out_rows = out.rearrange("(m p) n -> p m n", p=P)
+        units = S // UNIT
+        per_chunk = CHUNK // UNIT
+        x_codes = [gather_words(0)]
+        for u in range(units):
+            c, within = divmod(u, per_chunk)
+            cols = slice(within * UNIT, (within + 1) * UNIT)
+            if within == 0 and c + 1 < S // CHUNK:
+                x_codes.append(gather_words(c + 1))
+            acc1 = psum1.tile([P, PACK, UNIT], F32, name="acc1")
+            for t in range(PACK):
+                nc.tensor.matmul_mx(
+                    out=acc1[:, t, :],
+                    lhsT=w1_codes[:, t * P : (t + 1) * P].bitcast(FP8X4),
+                    lhsT_scale=w1_plane[:, t * P : (t + 1) * P],
+                    rhs=x_codes[c][:, cols].bitcast(FP8X4),
+                    rhs_scale=x_plane[:, u * UNIT : (u + 1) * UNIT],
+                    start=True,
+                    stop=True,
+                )
+            pre = work.tile([P, PACK, UNIT], F32, name="pre")
+            nc.vector.tensor_tensor(pre[:], acc1[:], pos_chunks[c][:, :, cols], ADD)
+            hidden = work.tile([P, UNIT, PACK], BF16, name="hidden", align_bytes=64)
+            nc.scalar.activation(
+                hidden[:].rearrange("p (c i) t -> p c t i", i=4),
+                pre[:].rearrange("p t (c i) -> p c t i", i=4),
+                GELU,
+            )
+            h_codes = work.tile([P, UNIT], U32, name="h_codes", align_bytes=64)
+            h_plane = work.tile([P, UNIT], U8, name="h_plane", align_bytes=64)
+            nc.vector.quantize_mx(out=h_codes[:].bitcast(FP8X4), scales=h_plane[:], in_=hidden[:].rearrange("p n t -> p (n t)"))
+            acc2 = psum2.tile([P, N // P, UNIT], F32, name="acc2")
+            for m in range(N // P):
+                nc.tensor.matmul_mx(
+                    out=acc2[:, m, :],
+                    lhsT=w2_codes[:, 2 * P * m : 2 * P * (m + 1)].bitcast(FP4X4),
+                    lhsT_scale=w2_plane[:, P * m : P * (m + 1)],
+                    rhs=h_codes[:].bitcast(FP8X4),
+                    rhs_scale=h_plane[:],
+                    start=True,
+                    stop=True,
+                )
+            if c == S // CHUNK - 1:
+                last = held.tile([P, N // P, UNIT], F32, name="last%d" % u)
+                if u >= units - VECTOR_COPIES:
+                    nc.vector.tensor_copy(last[:], acc2[:])
+                else:
+                    nc.scalar.copy(last[:], acc2[:])
+                nc.sync.dma_start(out_rows[:, :, u * UNIT : (u + 1) * UNIT], last[:])
+            else:
+                if within == 0:
+                    staged = held.tile([P, N // P, CHUNK], F32, name="staged%d" % c)
+                nc.scalar.copy(staged[:, :, cols], acc2[:])
+                if within == per_chunk - 1:
+                    nc.sync.dma_start(out_rows[:, :, c * CHUNK : (c + 1) * CHUNK], staged[:])

@@ -20,7 +20,8 @@ P = 128
 PACK = 4
 CHUNK = 256
 UNIT = 128
-VECTOR_COPIES = 1
+SECOND_LAG = 2
+OUT_LAG = 3
 
 
 def tile_picked_embpos_gelu_p_kernel(tc, x_words, x_scales, w1, w2_words, w2_scales, pos, offs, out):
@@ -28,8 +29,8 @@ def tile_picked_embpos_gelu_p_kernel(tc, x_words, x_scales, w1, w2_words, w2_sca
     with ExitStack() as ctx:
         held = ctx.enter_context(tc.tile_pool(name="held", bufs=1))
         work = ctx.enter_context(tc.tile_pool(name="work", bufs=4))
-        psum1 = ctx.enter_context(tc.psum_pool(name="psum1", bufs=5))
-        psum2 = ctx.enter_context(tc.psum_pool(name="psum2", bufs=3))
+        psum1 = ctx.enter_context(tc.psum_pool(name="psum1", bufs=4))
+        psum2 = ctx.enter_context(tc.psum_pool(name="psum2", bufs=4))
 
         w1_rows = w1.rearrange("(p j) c -> p j c", j=PACK)
         w1_raw = [held.tile([P, PACK, H // 2], F32, name="w1_raw%d" % half) for half in range(2)]
@@ -53,11 +54,12 @@ def tile_picked_embpos_gelu_p_kernel(tc, x_words, x_scales, w1, w2_words, w2_sca
         word_table = held.tile([P, T], U32, name="word_table", align_bytes=64)
         nc.sync.dma_start(word_table[:].bitcast(I32), x_words[0].rearrange("p n r -> p (n r)").bitcast(I32))
 
-        pos_rows = pos.rearrange("(p t) n -> p t n", t=PACK)
-        pos_chunks = []
         w2_codes = held.tile([P, 2 * N], U8, name="w2_codes", align_bytes=64)
         w2_plane = held.tile([P, N], U8, name="w2_plane", align_bytes=64)
         nc.vector.memset(w2_plane[:].bitcast(I32), 0)
+
+        pos_rows = pos.rearrange("(p t) n -> p t n", t=PACK)
+        pos_chunks = []
         for c in range(S // CHUNK):
             pos_chunk = held.tile([P, PACK, CHUNK], F32, name="pos_chunk%d" % c, tag="slot%d" % c, align_bytes=64)
             nc.sync.dma_start(pos_chunk[:], pos_rows[:, :, c * CHUNK : (c + 1) * CHUNK])
@@ -80,21 +82,24 @@ def tile_picked_embpos_gelu_p_kernel(tc, x_words, x_scales, w1, w2_words, w2_sca
         w1_plane = held.tile([P, H], U8, name="w1_plane", align_bytes=64)
         nc.vector.quantize_mx(out=w1_codes[:].bitcast(FP8X4), scales=w1_plane[:], in_=w1_grouped[:].rearrange("p t m j -> p (t m j)"))
 
-        def gather_words(c):
-            tag = "x_codes%d" % c if c < 2 else "slot%d" % (c - 2)
-            codes = held.tile([P, CHUNK], U32, name="x_codes%d" % c, tag=tag, align_bytes=64)
-            nc.vector.tensor_copy(codes[:], word_table[:].indirect(offsets[:, c * CHUNK // 16 : (c + 1) * CHUNK // 16]))
-            return codes
-
         out_rows = out.rearrange("(m p) n -> p m n", p=P)
         units = S // UNIT
+        chunks = S // CHUNK
         per_chunk = CHUNK // UNIT
-        x_codes = [gather_words(0)]
-        for u in range(units):
+        x_codes = {}
+        hidden = {}
+        acc2 = {}
+        staged = {}
+
+        def gather_words(first, count, tag):
+            codes = held.tile([P, count * CHUNK], U32, name="x_codes%d" % first, tag=tag, align_bytes=64)
+            nc.vector.tensor_copy(codes[:], word_table[:].indirect(offsets[:, first * CHUNK // 16 : (first + count) * CHUNK // 16]))
+            for i in range(count):
+                x_codes.setdefault(first + i, codes[:, i * CHUNK : (i + 1) * CHUNK])
+
+        def first_layer(u):
             c, within = divmod(u, per_chunk)
             cols = slice(within * UNIT, (within + 1) * UNIT)
-            if within == 0 and c + 1 < S // CHUNK:
-                x_codes.append(gather_words(c + 1))
             acc1 = psum1.tile([P, PACK, UNIT], F32, name="acc1")
             for t in range(PACK):
                 nc.tensor.matmul_mx(
@@ -108,19 +113,22 @@ def tile_picked_embpos_gelu_p_kernel(tc, x_words, x_scales, w1, w2_words, w2_sca
                 )
             pre = work.tile([P, PACK, UNIT], F32, name="pre")
             nc.vector.tensor_tensor(pre[:], acc1[:], pos_chunks[c][:, :, cols], ADD)
-            hidden = work.tile([P, UNIT, PACK], BF16, name="hidden", align_bytes=64)
+            h = work.tile([P, UNIT, PACK], BF16, name="h", align_bytes=64)
             nc.scalar.activation(
-                hidden[:].rearrange("p (c i) t -> p c t i", i=4),
+                h[:].rearrange("p (c i) t -> p c t i", i=4),
                 pre[:].rearrange("p t (c i) -> p c t i", i=4),
                 GELU,
             )
+            hidden.setdefault(u, h)
+
+        def second_layer(u):
             h_codes = work.tile([P, UNIT], U32, name="h_codes", align_bytes=64)
             h_plane = work.tile([P, UNIT], U8, name="h_plane", align_bytes=64)
-            nc.vector.quantize_mx(out=h_codes[:].bitcast(FP8X4), scales=h_plane[:], in_=hidden[:].rearrange("p n t -> p (n t)"))
-            acc2 = psum2.tile([P, N // P, UNIT], F32, name="acc2")
+            nc.vector.quantize_mx(out=h_codes[:].bitcast(FP8X4), scales=h_plane[:], in_=hidden[u][:].rearrange("p n t -> p (n t)"))
+            acc = psum2.tile([P, N // P, UNIT], F32, name="acc2")
             for m in range(N // P):
                 nc.tensor.matmul_mx(
-                    out=acc2[:, m, :],
+                    out=acc[:, m, :],
                     lhsT=w2_codes[:, 2 * P * m : 2 * P * (m + 1)].bitcast(FP4X4),
                     lhsT_scale=w2_plane[:, P * m : P * (m + 1)],
                     rhs=h_codes[:].bitcast(FP8X4),
@@ -128,16 +136,32 @@ def tile_picked_embpos_gelu_p_kernel(tc, x_words, x_scales, w1, w2_words, w2_sca
                     start=True,
                     stop=True,
                 )
-            if c == S // CHUNK - 1:
+            acc2.setdefault(u, acc)
+
+        def hand_out(u):
+            c, within = divmod(u, per_chunk)
+            if c == chunks - 1:
                 last = held.tile([P, N // P, UNIT], F32, name="last%d" % u)
-                if u >= units - VECTOR_COPIES:
-                    nc.vector.tensor_copy(last[:], acc2[:])
+                if u == units - 1:
+                    nc.vector.tensor_copy(last[:], acc2[u][:])
                 else:
-                    nc.scalar.copy(last[:], acc2[:])
+                    nc.scalar.copy(last[:], acc2[u][:])
                 nc.sync.dma_start(out_rows[:, :, u * UNIT : (u + 1) * UNIT], last[:])
             else:
                 if within == 0:
-                    staged = held.tile([P, N // P, CHUNK], F32, name="staged%d" % c)
-                nc.scalar.copy(staged[:, :, cols], acc2[:])
+                    staged.setdefault(c, held.tile([P, N // P, CHUNK], F32, name="staged%d" % c))
+                nc.scalar.copy(staged[c][:, :, within * UNIT : (within + 1) * UNIT], acc2[u][:])
                 if within == per_chunk - 1:
-                    nc.sync.dma_start(out_rows[:, :, c * CHUNK : (c + 1) * CHUNK], staged[:])
+                    nc.sync.dma_start(out_rows[:, :, c * CHUNK : (c + 1) * CHUNK], staged[c][:])
+
+        gather_words(0, 1, "first_codes")
+        gather_words(1, 2, "middle_codes")
+        for step in range(units + OUT_LAG):
+            if step < units:
+                first_layer(step)
+            if step == per_chunk - 1:
+                gather_words(3, 1, "slot0")
+            if SECOND_LAG <= step < units + SECOND_LAG:
+                second_layer(step - SECOND_LAG)
+            if step >= OUT_LAG:
+                hand_out(step - OUT_LAG)

@@ -72,15 +72,32 @@ def tile_picked_embpos_gelu_p_kernel(tc, x_words, x_scales, w1, w2_words, w2_sca
         x_plane = held.tile([P, S], U8, name="x_plane", align_bytes=64)
         nc.vector.tensor_copy(x_plane[:], scale_table[:].indirect(offsets[:]))
 
-        w1_grouped = held.tile([P, PACK, P, PACK], BF16, name="w1_grouped", align_bytes=64)
+        w1_grouped = [held.tile([P, 2, P, PACK], BF16, name="w1_grouped%d" % pair, align_bytes=64) for pair in range(2)]
         for half in range(2):
-            nc.scalar.copy(
-                w1_grouped[:, :, half * P // 2 : (half + 1) * P // 2, :].rearrange("p t m j -> p m j t"),
-                w1_raw[half][:].rearrange("p j (m t) -> p m j t", t=PACK),
-            )
+            for pair in range(2):
+                nc.scalar.copy(
+                    w1_grouped[pair][:, :, half * P // 2 : (half + 1) * P // 2, :].rearrange("p t m j -> p m j t"),
+                    w1_raw[half][:].rearrange("p j (m t) -> p m j t", t=PACK)[:, :, :, 2 * pair : 2 * pair + 2],
+                )
         w1_codes = held.tile([P, H], U32, name="w1_codes", align_bytes=64)
         w1_plane = held.tile([P, H], U8, name="w1_plane", align_bytes=64)
-        nc.vector.quantize_mx(out=w1_codes[:].bitcast(FP8X4), scales=w1_plane[:], in_=w1_grouped[:].rearrange("p t m j -> p (t m j)"))
+        for pair in range(2):
+            nc.vector.quantize_mx(
+                out=w1_codes[:, 2 * pair * P : 2 * (pair + 1) * P].bitcast(FP8X4),
+                scales=w1_plane[:, 2 * pair * P : 2 * (pair + 1) * P],
+                in_=w1_grouped[pair][:].rearrange("p t m j -> p (t m j)"),
+            )
+        warm_bank = psum2.tile([P, 2, CHUNK], F32, name="warm_bank", tag="acc2")
+        for i in range(4):
+            nc.tensor.matmul_mx(
+                out=warm_bank[:, i % 2, :],
+                lhsT=w1_codes[:, :P].bitcast(FP8X4),
+                lhsT_scale=w1_plane[:, :P],
+                rhs=w1_codes[:, :CHUNK].bitcast(FP8X4),
+                rhs_scale=w1_plane[:, :CHUNK],
+                start=True,
+                stop=True,
+            )
 
         out_rows = out.rearrange("(m p) n -> p m n", p=P)
         units = S // UNIT

@@ -20,17 +20,14 @@ P = 128
 PACK = 4
 CHUNK = 256
 UNIT = 128
-SECOND_LAG = 2
-OUT_LAG = 3
 
 
 def tile_picked_embpos_gelu_p_kernel(tc, x_words, x_scales, w1, w2_words, w2_scales, pos, offs, out):
     nc = tc.nc
     with ExitStack() as ctx:
         held = ctx.enter_context(tc.tile_pool(name="held", bufs=1))
-        work = ctx.enter_context(tc.tile_pool(name="work", bufs=4))
-        psum1 = ctx.enter_context(tc.psum_pool(name="psum1", bufs=4))
-        psum2 = ctx.enter_context(tc.psum_pool(name="psum2", bufs=4))
+        psum1 = ctx.enter_context(tc.psum_pool(name="psum1", bufs=1))
+        psum2 = ctx.enter_context(tc.psum_pool(name="psum2", bufs=1))
 
         w1_rows = w1.rearrange("(p j) c -> p j c", j=PACK)
         w1_raw = [held.tile([P, PACK, H // 2], F32, name="w1_raw%d" % half) for half in range(2)]
@@ -44,10 +41,10 @@ def tile_picked_embpos_gelu_p_kernel(tc, x_words, x_scales, w1, w2_words, w2_sca
         for q in range(4):
             nc.sync.dma_start(scale_table[32 * q : 32 * q + 4, :].bitcast(I32), x_scales[0, 4 * q : 4 * q + 4, :].bitcast(I32))
 
-        warm_in = held.tile([P, 8], F32, name="warm_in")
-        warm_out = held.tile([P, 8], F32, name="warm_out")
-        nc.vector.memset(warm_in[:], 0.0)
-        nc.scalar.activation(warm_out[:], warm_in[:], GELU)
+        zero_in = held.tile([P, 1], F32, name="zero_in")
+        zero_bias = held.tile([P, 1], F32, name="zero_bias")
+        nc.vector.memset(zero_in[:], 0.0)
+        nc.scalar.activation(zero_bias[:], zero_in[:], GELU)
 
         nc.sync.dma_start(w1_raw[1][:], w1_rows[:, :, H // 2 :])
 
@@ -72,41 +69,24 @@ def tile_picked_embpos_gelu_p_kernel(tc, x_words, x_scales, w1, w2_words, w2_sca
         x_plane = held.tile([P, S], U8, name="x_plane", align_bytes=64)
         nc.vector.tensor_copy(x_plane[:], scale_table[:].indirect(offsets[:]))
 
-        w1_grouped = [held.tile([P, 2, P, PACK], BF16, name="w1_grouped%d" % pair, align_bytes=64) for pair in range(2)]
+        w1_grouped = held.tile([P, PACK, P, PACK], BF16, name="w1_grouped", align_bytes=64)
         for half in range(2):
-            for pair in range(2):
-                nc.scalar.copy(
-                    w1_grouped[pair][:, :, half * P // 2 : (half + 1) * P // 2, :].rearrange("p t m j -> p m j t"),
-                    w1_raw[half][:].rearrange("p j (m t) -> p m j t", t=PACK)[:, :, :, 2 * pair : 2 * pair + 2],
-                )
+            nc.scalar.copy(
+                w1_grouped[:, :, half * P // 2 : (half + 1) * P // 2, :].rearrange("p t m j -> p m j t"),
+                w1_raw[half][:].rearrange("p j (m t) -> p m j t", t=PACK),
+            )
         w1_codes = held.tile([P, H], U32, name="w1_codes", align_bytes=64)
         w1_plane = held.tile([P, H], U8, name="w1_plane", align_bytes=64)
-        for pair in range(2):
-            nc.vector.quantize_mx(
-                out=w1_codes[:, 2 * pair * P : 2 * (pair + 1) * P].bitcast(FP8X4),
-                scales=w1_plane[:, 2 * pair * P : 2 * (pair + 1) * P],
-                in_=w1_grouped[pair][:].rearrange("p t m j -> p (t m j)"),
-            )
-        warm_bank = psum2.tile([P, 2, CHUNK], F32, name="warm_bank", tag="acc2")
-        for i in range(4):
-            nc.tensor.matmul_mx(
-                out=warm_bank[:, i % 2, :],
-                lhsT=w1_codes[:, :P].bitcast(FP8X4),
-                lhsT_scale=w1_plane[:, :P],
-                rhs=w1_codes[:, :CHUNK].bitcast(FP8X4),
-                rhs_scale=w1_plane[:, :CHUNK],
-                start=True,
-                stop=True,
-            )
+        nc.vector.quantize_mx(out=w1_codes[:].bitcast(FP8X4), scales=w1_plane[:], in_=w1_grouped[:].rearrange("p t m j -> p (t m j)"))
 
         out_rows = out.rearrange("(m p) n -> p m n", p=P)
         units = S // UNIT
-        chunks = S // CHUNK
         per_chunk = CHUNK // UNIT
         x_codes = {}
-        hidden = {}
-        acc2 = {}
-        staged = {}
+        banks1 = [psum1.tile([P, PACK, UNIT], F32, name="acc1_%d" % b) for b in range(4)]
+        banks2 = [psum2.tile([P, N // P, UNIT], F32, name="acc2_%d" % b) for b in range(4)]
+        hidden = [held.tile([P, UNIT, PACK], BF16, name="h%d" % u, tag="h_slot%d" % u, align_bytes=64) for u in range(units)]
+        sums = [held.tile([P, PACK, UNIT], F32, name="pre%d" % u, tag="pre_slot%d" % u, align_bytes=64) for u in range(units)]
 
         def gather_words(first, count, tag):
             codes = held.tile([P, count * CHUNK], U32, name="x_codes%d" % first, tag=tag, align_bytes=64)
@@ -117,10 +97,9 @@ def tile_picked_embpos_gelu_p_kernel(tc, x_words, x_scales, w1, w2_words, w2_sca
         def first_layer(u):
             c, within = divmod(u, per_chunk)
             cols = slice(within * UNIT, (within + 1) * UNIT)
-            acc1 = psum1.tile([P, PACK, UNIT], F32, name="acc1")
             for t in range(PACK):
                 nc.tensor.matmul_mx(
-                    out=acc1[:, t, :],
+                    out=banks1[u % 4][:, t, :],
                     lhsT=w1_codes[:, t * P : (t + 1) * P].bitcast(FP8X4),
                     lhsT_scale=w1_plane[:, t * P : (t + 1) * P],
                     rhs=x_codes[c][:, cols].bitcast(FP8X4),
@@ -128,24 +107,41 @@ def tile_picked_embpos_gelu_p_kernel(tc, x_words, x_scales, w1, w2_words, w2_sca
                     start=True,
                     stop=True,
                 )
-            pre = work.tile([P, PACK, UNIT], F32, name="pre")
-            nc.vector.tensor_tensor(pre[:], acc1[:], pos_chunks[c][:, :, cols], ADD)
-            h = work.tile([P, UNIT, PACK], BF16, name="h", align_bytes=64)
-            nc.scalar.activation(
-                h[:].rearrange("p (c i) t -> p c t i", i=4),
-                pre[:].rearrange("p t (c i) -> p c t i", i=4),
-                GELU,
-            )
-            hidden.setdefault(u, h)
 
-        def second_layer(u):
-            h_codes = work.tile([P, UNIT], U32, name="h_codes", align_bytes=64)
-            h_plane = work.tile([P, UNIT], U8, name="h_plane", align_bytes=64)
+        def gelu(u, lo, hi):
+            nc.scalar.activation(
+                hidden[u][:, lo:hi, :].rearrange("p (c i) t -> p c t i", i=4),
+                sums[u][:, :, lo:hi].rearrange("p t (c i) -> p c t i", i=4),
+                GELU,
+                bias=zero_bias[:],
+            )
+
+        def activate(u):
+            c, within = divmod(u, per_chunk)
+            at = within * UNIT
+            if u == units - 1 and False:
+                for lo in (0, UNIT // 2):
+                    hi = lo + UNIT // 2
+                    nc.vector.tensor_tensor(sums[u][:, :, lo:hi], banks1[u % 4][:, :, lo:hi], pos_chunks[c][:, :, at + lo : at + hi], ADD)
+                    gelu(u, lo, hi)
+            else:
+                nc.vector.tensor_tensor(sums[u][:], banks1[u % 4][:], pos_chunks[c][:, :, at : at + UNIT], ADD)
+                gelu(u, 0, UNIT)
+            if u < 2:
+                first_layer(u + 4)
+
+        def result_bank(u, m):
+            if u == units - 1 and m == 1:
+                return banks1[0][:, 0, :]
+            return banks2[u % 4][:, m, :]
+
+        def second_layer(u, tag):
+            h_codes = held.tile([P, UNIT], U32, name="h_codes%d" % u, tag=tag, align_bytes=64)
+            h_plane = held.tile([P, UNIT], U8, name="h_plane%d" % u, align_bytes=64)
             nc.vector.quantize_mx(out=h_codes[:].bitcast(FP8X4), scales=h_plane[:], in_=hidden[u][:].rearrange("p n t -> p (n t)"))
-            acc = psum2.tile([P, N // P, UNIT], F32, name="acc2")
             for m in range(N // P):
                 nc.tensor.matmul_mx(
-                    out=acc[:, m, :],
+                    out=result_bank(u, m),
                     lhsT=w2_codes[:, 2 * P * m : 2 * P * (m + 1)].bitcast(FP4X4),
                     lhsT_scale=w2_plane[:, P * m : P * (m + 1)],
                     rhs=h_codes[:].bitcast(FP8X4),
@@ -153,32 +149,54 @@ def tile_picked_embpos_gelu_p_kernel(tc, x_words, x_scales, w1, w2_words, w2_sca
                     start=True,
                     stop=True,
                 )
-            acc2.setdefault(u, acc)
 
-        def hand_out(u):
-            c, within = divmod(u, per_chunk)
-            if c == chunks - 1:
-                last = held.tile([P, N // P, UNIT], F32, name="last%d" % u)
-                if u == units - 1:
-                    nc.vector.tensor_copy(last[:], acc2[u][:])
-                else:
-                    nc.scalar.copy(last[:], acc2[u][:])
-                nc.sync.dma_start(out_rows[:, :, u * UNIT : (u + 1) * UNIT], last[:])
+        groups = ((0, 3), (3, 5), (5, 7), (7, 8))
+        staged = {}
+        stage_tags = {3: "slot3"}
+
+        def hand_out(u, on_vector):
+            first, last = [g for g in groups if g[0] <= u < g[1]][0]
+            if first not in staged:
+                staged.setdefault(first, held.tile([P, N // P, (last - first) * UNIT], F32, name="staged%d" % first, tag=stage_tags.get(first, "stage%d" % first), align_bytes=64))
+            into = staged[first][:, :, (u - first) * UNIT : (u - first + 1) * UNIT]
+            if u == units - 1:
+                nc.scalar.copy(into[:, 0, :], result_bank(u, 0))
+                nc.vector.tensor_copy(into[:, 1, :], result_bank(u, 1))
+            elif on_vector:
+                nc.vector.tensor_copy(into, banks2[u % 4][:])
             else:
-                if within == 0:
-                    staged.setdefault(c, held.tile([P, N // P, CHUNK], F32, name="staged%d" % c))
-                nc.scalar.copy(staged[c][:, :, within * UNIT : (within + 1) * UNIT], acc2[u][:])
-                if within == per_chunk - 1:
-                    nc.sync.dma_start(out_rows[:, :, c * CHUNK : (c + 1) * CHUNK], staged[c][:])
+                nc.scalar.copy(into, banks2[u % 4][:])
+            if u == last - 1:
+                nc.sync.dma_start(out_rows[:, :, first * UNIT : last * UNIT], staged[first][:])
 
         gather_words(0, 1, "first_codes")
         gather_words(1, 2, "middle_codes")
-        for step in range(units + OUT_LAG):
-            if step < units:
-                first_layer(step)
-            if step == per_chunk - 1:
-                gather_words(3, 1, "slot0")
-            if SECOND_LAG <= step < units + SECOND_LAG:
-                second_layer(step - SECOND_LAG)
-            if step >= OUT_LAG:
-                hand_out(step - OUT_LAG)
+        for u in range(4):
+            first_layer(u)
+        activate(0)
+        activate(1)
+        activate(2)
+        activate(3)
+        activate(4)
+        second_layer(0, "pre_slot2")
+        second_layer(1, "pre_slot3")
+        gather_words(3, 1, "slot1")
+        first_layer(6)
+        first_layer(7)
+        hand_out(0, False)
+        hand_out(1, False)
+        activate(5)
+        second_layer(2, "codes2")
+        second_layer(3, "codes3")
+        second_layer(4, "codes4")
+        hand_out(2, False)
+        activate(6)
+        activate(7)
+        second_layer(5, "codes5")
+        second_layer(6, "codes6")
+        hand_out(3, True)
+        second_layer(7, "codes7")
+        hand_out(4, False)
+        hand_out(5, False)
+        hand_out(6, False)
+        hand_out(7, True)

@@ -119,7 +119,7 @@ def tile_picked_embpos_gelu_p_kernel(tc, x_words, x_scales, w1, w2_words, w2_sca
         def activate(u):
             c, within = divmod(u, per_chunk)
             at = within * UNIT
-            if u == units - 1 and False:
+            if u >= units - 2:
                 for lo in (0, UNIT // 2):
                     hi = lo + UNIT // 2
                     nc.vector.tensor_tensor(sums[u][:, :, lo:hi], banks1[u % 4][:, :, lo:hi], pos_chunks[c][:, :, at + lo : at + hi], ADD)
@@ -150,7 +150,7 @@ def tile_picked_embpos_gelu_p_kernel(tc, x_words, x_scales, w1, w2_words, w2_sca
                     stop=True,
                 )
 
-        groups = ((0, 3), (3, 5), (5, 7), (7, 8))
+        groups = ((0, 3), (3, 5), (5, 6), (6, 7), (7, 8))
         staged = {}
         stage_tags = {3: "slot3"}
 

@@ -38,8 +38,8 @@ def tile_picked_embpos_gelu_p_kernel(tc, x_words, x_scales, w1, w2_words, w2_sca
 
         scale_table = held.tile([P, T], U8, name="scale_table", align_bytes=64)
         nc.vector.memset(scale_table[:].bitcast(I32), 0)
-        for q in range(4):
-            nc.sync.dma_start(scale_table[32 * q : 32 * q + 4, :].bitcast(I32), x_scales[0, 4 * q : 4 * q + 4, :].bitcast(I32))
+        for r in range(PACK):
+            nc.sync.dma_start(scale_table[r:P:32, :].bitcast(I32), x_scales[0, r::PACK, :].bitcast(I32))
 
         zero_in = held.tile([P, 1], F32, name="zero_in")
         zero_bias = held.tile([P, 1], F32, name="zero_bias")
@@ -63,8 +63,8 @@ def tile_picked_embpos_gelu_p_kernel(tc, x_words, x_scales, w1, w2_words, w2_sca
             pos_chunks.append(pos_chunk)
             if c == 0:
                 nc.sync.dma_start(w2_codes[:].bitcast(I32), w2_words[0].bitcast(I32))
-                for q in range(4):
-                    nc.sync.dma_start(w2_plane[32 * q : 32 * q + 4, :].bitcast(I32), w2_scales[0, 4 * q : 4 * q + 4, :].bitcast(I32))
+                for r in range(PACK):
+                    nc.sync.dma_start(w2_plane[r:P:32, :].bitcast(I32), w2_scales[0, r::PACK, :].bitcast(I32))
 
         x_plane = held.tile([P, S], U8, name="x_plane", align_bytes=64)
         nc.vector.tensor_copy(x_plane[:], scale_table[:].indirect(offsets[:]))

@@ -150,9 +150,9 @@ def tile_picked_embpos_gelu_p_kernel(tc, x_words, x_scales, w1, w2_words, w2_sca
                     stop=True,
                 )
 
-        groups = ((0, 3), (3, 5), (5, 6), (6, 7), (7, 8))
+        groups = ((0, 2), (2, 4), (4, 5), (5, 6), (6, 7), (7, 8))
         staged = {}
-        stage_tags = {3: "slot3"}
+        stage_tags = {4: "slot3"}
 
         def hand_out(u, on_vector):
             first, last = [g for g in groups if g[0] <= u < g[1]][0]
@@ -166,7 +166,10 @@ def tile_picked_embpos_gelu_p_kernel(tc, x_words, x_scales, w1, w2_words, w2_sca
                 nc.vector.tensor_copy(into, banks2[u % 4][:])
             else:
                 nc.scalar.copy(into, banks2[u % 4][:])
-            if u == last - 1:
+            if u == units - 1:
+                nc.scalar.dma_start(out_rows[:, 0, u * UNIT :], into[:, 0, :])
+                nc.sync.dma_start(out_rows[:, 1, u * UNIT :], into[:, 1, :])
+            elif u == last - 1:
                 nc.sync.dma_start(out_rows[:, :, first * UNIT : last * UNIT], staged[first][:])
 
         gather_words(0, 1, "first_codes")
@@ -180,23 +183,23 @@ def tile_picked_embpos_gelu_p_kernel(tc, x_words, x_scales, w1, w2_words, w2_sca
         activate(4)
         second_layer(0, "pre_slot2")
         second_layer(1, "pre_slot3")
+        second_layer(2, "codes2")
         gather_words(3, 1, "slot1")
         first_layer(6)
         first_layer(7)
         hand_out(0, False)
         hand_out(1, False)
+        hand_out(2, False)
         activate(5)
-        second_layer(2, "codes2")
         second_layer(3, "codes3")
         second_layer(4, "codes4")
-        hand_out(2, False)
+        hand_out(3, False)
         activate(6)
         activate(7)
         second_layer(5, "codes5")
         second_layer(6, "codes6")
-        hand_out(3, True)
+        hand_out(4, True)
         second_layer(7, "codes7")
-        hand_out(4, False)
         hand_out(5, False)
         hand_out(6, False)
         hand_out(7, True)

@@ -26,6 +26,7 @@ def tile_picked_embpos_gelu_p_kernel(tc, x_words, x_scales, w1, w2_words, w2_sca
     nc = tc.nc
     with ExitStack() as ctx:
         held = ctx.enter_context(tc.tile_pool(name="held", bufs=1))
+        late = ctx.enter_context(tc.tile_pool(name="late", bufs=1))
         psum1 = ctx.enter_context(tc.psum_pool(name="psum1", bufs=1))
         psum2 = ctx.enter_context(tc.psum_pool(name="psum2", bufs=1))
 
@@ -58,7 +59,10 @@ def tile_picked_embpos_gelu_p_kernel(tc, x_words, x_scales, w1, w2_words, w2_sca
         pos_rows = pos.rearrange("(p t) n -> p t n", t=PACK)
         pos_chunks = []
         for c in range(S // CHUNK):
-            pos_chunk = held.tile([P, PACK, CHUNK], F32, name="pos_chunk%d" % c, tag="slot%d" % c, align_bytes=64)
+            if c == S // CHUNK - 1:
+                pos_chunk = late.tile([P, PACK, CHUNK], F32, name="pos_chunk%d" % c, align_bytes=64, offset=0)
+            else:
+                pos_chunk = held.tile([P, PACK, CHUNK], F32, name="pos_chunk%d" % c, tag="slot%d" % c, align_bytes=64)
             nc.sync.dma_start(pos_chunk[:], pos_rows[:, :, c * CHUNK : (c + 1) * CHUNK])
             pos_chunks.append(pos_chunk)
             if c == 0:
@@ -150,12 +154,14 @@ def tile_picked_embpos_gelu_p_kernel(tc, x_words, x_scales, w1, w2_words, w2_sca
                     stop=True,
                 )
 
-        groups = ((0, 2), (2, 4), (4, 5), (5, 6), (6, 7), (7, 8))
+        groups = ((0, 3), (3, 4), (4, 5), (5, 6), (6, 7), (7, 8))
         staged = {}
-        stage_tags = {4: "slot3"}
+        stage_tags = {6: "h_slot7"}
 
         def hand_out(u, on_vector):
             first, last = [g for g in groups if g[0] <= u < g[1]][0]
+            if first in (3, 4):
+                staged.setdefault(first, late.tile([P, N // P, UNIT], F32, name="staged%d" % first, align_bytes=64, offset=(first - 3) * 1024))
             if first not in staged:
                 staged.setdefault(first, held.tile([P, N // P, (last - first) * UNIT], F32, name="staged%d" % first, tag=stage_tags.get(first, "stage%d" % first), align_bytes=64))
             into = staged[first][:, :, (u - first) * UNIT : (u - first + 1) * UNIT]
@@ -167,7 +173,7 @@ def tile_picked_embpos_gelu_p_kernel(tc, x_words, x_scales, w1, w2_words, w2_sca
             else:
                 nc.scalar.copy(into, banks2[u % 4][:])
             if u == units - 1:
-                nc.scalar.dma_start(out_rows[:, 0, u * UNIT :], into[:, 0, :])
+                nc.sync.dma_start(out_rows[:, 0, u * UNIT :], into[:, 0, :])
                 nc.sync.dma_start(out_rows[:, 1, u * UNIT :], into[:, 1, :])
             elif u == last - 1:
                 nc.sync.dma_start(out_rows[:, :, first * UNIT : last * UNIT], staged[first][:])
@@ -193,13 +199,13 @@ def tile_picked_embpos_gelu_p_kernel(tc, x_words, x_scales, w1, w2_words, w2_sca
         activate(5)
         second_layer(3, "codes3")
         second_layer(4, "codes4")
-        hand_out(3, False)
         activate(6)
         activate(7)
         second_layer(5, "codes5")
         second_layer(6, "codes6")
-        hand_out(4, True)
+        hand_out(3, True)
         second_layer(7, "codes7")
+        hand_out(4, False)
         hand_out(5, False)
-        hand_out(6, False)
+        hand_out(6, True)
         hand_out(7, True)

@@ -18,8 +18,15 @@ ADD = mybir.AluOpType.add
 
 P = 128
 PACK = 4
-CHUNK = 256
+QUADRANT = 32
+LIST_ROWS = 16
 UNIT = 128
+CHUNK = 256
+UNITS = S // UNIT
+BANKS = 4
+HALVED_FROM = UNITS - 2
+STORE_GROUPS = ((0, 3), (3, 4), (4, 5), (5, 6), (6, 7), (7, 8))
+STAGE_BYTES = N // P * UNIT * 4
 
 
 def tile_picked_embpos_gelu_p_kernel(tc, x_words, x_scales, w1, w2_words, w2_scales, pos, offs, out):
@@ -30,17 +37,20 @@ def tile_picked_embpos_gelu_p_kernel(tc, x_words, x_scales, w1, w2_words, w2_sca
         psum1 = ctx.enter_context(tc.psum_pool(name="psum1", bufs=1))
         psum2 = ctx.enter_context(tc.psum_pool(name="psum2", bufs=1))
 
+        def load_scale_rows(plane, rows):
+            for r in range(PACK):
+                nc.sync.dma_start(plane[r:P:QUADRANT, :].bitcast(I32), rows[r::PACK, :].bitcast(I32))
+
         w1_rows = w1.rearrange("(p j) c -> p j c", j=PACK)
         w1_raw = [held.tile([P, PACK, H // 2], F32, name="w1_raw%d" % half) for half in range(2)]
         nc.sync.dma_start(w1_raw[0][:], w1_rows[:, :, : H // 2])
 
-        offsets = held.tile([P, S // 16], U16, name="offsets")
+        offsets = held.tile([P, S // LIST_ROWS], U16, name="offsets")
         nc.sync.dma_start(offsets[:], offs)
 
         scale_table = held.tile([P, T], U8, name="scale_table", align_bytes=64)
         nc.vector.memset(scale_table[:].bitcast(I32), 0)
-        for r in range(PACK):
-            nc.sync.dma_start(scale_table[r:P:32, :].bitcast(I32), x_scales[0, r::PACK, :].bitcast(I32))
+        load_scale_rows(scale_table, x_scales[0])
 
         zero_in = held.tile([P, 1], F32, name="zero_in")
         zero_bias = held.tile([P, 1], F32, name="zero_bias")
@@ -62,13 +72,12 @@ def tile_picked_embpos_gelu_p_kernel(tc, x_words, x_scales, w1, w2_words, w2_sca
             if c == S // CHUNK - 1:
                 pos_chunk = late.tile([P, PACK, CHUNK], F32, name="pos_chunk%d" % c, align_bytes=64, offset=0)
             else:
-                pos_chunk = held.tile([P, PACK, CHUNK], F32, name="pos_chunk%d" % c, tag="slot%d" % c, align_bytes=64)
+                pos_chunk = held.tile([P, PACK, CHUNK], F32, name="pos_chunk%d" % c, tag="pos%d" % c, align_bytes=64)
             nc.sync.dma_start(pos_chunk[:], pos_rows[:, :, c * CHUNK : (c + 1) * CHUNK])
             pos_chunks.append(pos_chunk)
             if c == 0:
                 nc.sync.dma_start(w2_codes[:].bitcast(I32), w2_words[0].bitcast(I32))
-                for r in range(PACK):
-                    nc.sync.dma_start(w2_plane[r:P:32, :].bitcast(I32), w2_scales[0, r::PACK, :].bitcast(I32))
+                load_scale_rows(w2_plane, w2_scales[0])
 
         x_plane = held.tile([P, S], U8, name="x_plane", align_bytes=64)
         nc.vector.tensor_copy(x_plane[:], scale_table[:].indirect(offsets[:]))
@@ -84,17 +93,16 @@ def tile_picked_embpos_gelu_p_kernel(tc, x_words, x_scales, w1, w2_words, w2_sca
         nc.vector.quantize_mx(out=w1_codes[:].bitcast(FP8X4), scales=w1_plane[:], in_=w1_grouped[:].rearrange("p t m j -> p (t m j)"))
 
         out_rows = out.rearrange("(m p) n -> p m n", p=P)
-        units = S // UNIT
         per_chunk = CHUNK // UNIT
         x_codes = {}
-        banks1 = [psum1.tile([P, PACK, UNIT], F32, name="acc1_%d" % b) for b in range(4)]
-        banks2 = [psum2.tile([P, N // P, UNIT], F32, name="acc2_%d" % b) for b in range(4)]
-        hidden = [held.tile([P, UNIT, PACK], BF16, name="h%d" % u, tag="h_slot%d" % u, align_bytes=64) for u in range(units)]
-        sums = [held.tile([P, PACK, UNIT], F32, name="pre%d" % u, tag="pre_slot%d" % u, align_bytes=64) for u in range(units)]
+        banks1 = [psum1.tile([P, PACK, UNIT], F32, name="acc1_%d" % b) for b in range(BANKS)]
+        banks2 = [psum2.tile([P, N // P, UNIT], F32, name="acc2_%d" % b) for b in range(BANKS)]
+        hidden = [held.tile([P, UNIT, PACK], BF16, name="h%d" % u, tag="hidden%d" % u, align_bytes=64) for u in range(UNITS)]
+        sums = [held.tile([P, PACK, UNIT], F32, name="pre%d" % u, tag="sum%d" % u, align_bytes=64) for u in range(UNITS)]
 
         def gather_words(first, count, tag):
             codes = held.tile([P, count * CHUNK], U32, name="x_codes%d" % first, tag=tag, align_bytes=64)
-            nc.vector.tensor_copy(codes[:], word_table[:].indirect(offsets[:, first * CHUNK // 16 : (first + count) * CHUNK // 16]))
+            nc.vector.tensor_copy(codes[:], word_table[:].indirect(offsets[:, first * CHUNK // LIST_ROWS : (first + count) * CHUNK // LIST_ROWS]))
             for i in range(count):
                 x_codes.setdefault(first + i, codes[:, i * CHUNK : (i + 1) * CHUNK])
 
@@ -103,7 +111,7 @@ def tile_picked_embpos_gelu_p_kernel(tc, x_words, x_scales, w1, w2_words, w2_sca
             cols = slice(within * UNIT, (within + 1) * UNIT)
             for t in range(PACK):
                 nc.tensor.matmul_mx(
-                    out=banks1[u % 4][:, t, :],
+                    out=banks1[u % BANKS][:, t, :],
                     lhsT=w1_codes[:, t * P : (t + 1) * P].bitcast(FP8X4),
                     lhsT_scale=w1_plane[:, t * P : (t + 1) * P],
                     rhs=x_codes[c][:, cols].bitcast(FP8X4),
@@ -112,7 +120,10 @@ def tile_picked_embpos_gelu_p_kernel(tc, x_words, x_scales, w1, w2_words, w2_sca
                     stop=True,
                 )
 
-        def gelu(u, lo, hi):
+        def add_and_gelu(u, lo, hi):
+            c, within = divmod(u, per_chunk)
+            at = within * UNIT
+            nc.vector.tensor_tensor(sums[u][:, :, lo:hi], banks1[u % BANKS][:, :, lo:hi], pos_chunks[c][:, :, at + lo : at + hi], ADD)
             nc.scalar.activation(
                 hidden[u][:, lo:hi, :].rearrange("p (c i) t -> p c t i", i=4),
                 sums[u][:, :, lo:hi].rearrange("p t (c i) -> p c t i", i=4),
@@ -121,23 +132,14 @@ def tile_picked_embpos_gelu_p_kernel(tc, x_words, x_scales, w1, w2_words, w2_sca
             )
 
         def activate(u):
-            c, within = divmod(u, per_chunk)
-            at = within * UNIT
-            if u >= units - 2:
-                for lo in (0, UNIT // 2):
-                    hi = lo + UNIT // 2
-                    nc.vector.tensor_tensor(sums[u][:, :, lo:hi], banks1[u % 4][:, :, lo:hi], pos_chunks[c][:, :, at + lo : at + hi], ADD)
-                    gelu(u, lo, hi)
-            else:
-                nc.vector.tensor_tensor(sums[u][:], banks1[u % 4][:], pos_chunks[c][:, :, at : at + UNIT], ADD)
-                gelu(u, 0, UNIT)
-            if u < 2:
-                first_layer(u + 4)
+            width = UNIT // 2 if u >= HALVED_FROM else UNIT
+            for lo in range(0, UNIT, width):
+                add_and_gelu(u, lo, lo + width)
 
         def result_bank(u, m):
-            if u == units - 1 and m == 1:
+            if u == UNITS - 1 and m == 1:
                 return banks1[0][:, 0, :]
-            return banks2[u % 4][:, m, :]
+            return banks2[u % BANKS][:, m, :]
 
         def second_layer(u, tag):
             h_codes = held.tile([P, UNIT], U32, name="h_codes%d" % u, tag=tag, align_bytes=64)
@@ -154,58 +156,60 @@ def tile_picked_embpos_gelu_p_kernel(tc, x_words, x_scales, w1, w2_words, w2_sca
                     stop=True,
                 )
 
-        groups = ((0, 3), (3, 4), (4, 5), (5, 6), (6, 7), (7, 8))
-        staged = {}
-        stage_tags = {6: "h_slot7"}
-
-        def hand_out(u, on_vector):
-            first, last = [g for g in groups if g[0] <= u < g[1]][0]
+        def staging_tile(first, last):
+            shape = [P, N // P, (last - first) * UNIT]
             if first in (3, 4):
-                staged.setdefault(first, late.tile([P, N // P, UNIT], F32, name="staged%d" % first, align_bytes=64, offset=(first - 3) * 1024))
+                return late.tile(shape, F32, name="staged%d" % first, align_bytes=64, offset=(first - 3) * STAGE_BYTES)
+            tag = "sum%d" % (UNITS - 1) if first == UNITS - 2 else "stage%d" % first
+            return held.tile(shape, F32, name="staged%d" % first, tag=tag, align_bytes=64)
+
+        staged = {}
+
+        def hand_out(u, copy):
+            first, last = [g for g in STORE_GROUPS if g[0] <= u < g[1]][0]
             if first not in staged:
-                staged.setdefault(first, held.tile([P, N // P, (last - first) * UNIT], F32, name="staged%d" % first, tag=stage_tags.get(first, "stage%d" % first), align_bytes=64))
-            into = staged[first][:, :, (u - first) * UNIT : (u - first + 1) * UNIT]
-            if u == units - 1:
-                nc.scalar.copy(into[:, 0, :], result_bank(u, 0))
-                nc.vector.tensor_copy(into[:, 1, :], result_bank(u, 1))
-            elif on_vector:
-                nc.vector.tensor_copy(into, banks2[u % 4][:])
-            else:
-                nc.scalar.copy(into, banks2[u % 4][:])
-            if u == units - 1:
-                nc.sync.dma_start(out_rows[:, 0, u * UNIT :], into[:, 0, :])
-                nc.sync.dma_start(out_rows[:, 1, u * UNIT :], into[:, 1, :])
-            elif u == last - 1:
+                staged.setdefault(first, staging_tile(first, last))
+            copy(staged[first][:, :, (u - first) * UNIT : (u - first + 1) * UNIT], banks2[u % BANKS][:])
+            if u == last - 1:
                 nc.sync.dma_start(out_rows[:, :, first * UNIT : last * UNIT], staged[first][:])
+
+        def hand_out_last():
+            u = UNITS - 1
+            tile = staging_tile(u, UNITS)
+            nc.scalar.copy(tile[:, 0, :], result_bank(u, 0))
+            nc.vector.tensor_copy(tile[:, 1, :], result_bank(u, 1))
+            for m in range(N // P):
+                nc.sync.dma_start(out_rows[:, m, u * UNIT :], tile[:, m, :])
 
         gather_words(0, 1, "first_codes")
         gather_words(1, 2, "middle_codes")
-        for u in range(4):
+        for u in range(BANKS):
             first_layer(u)
-        activate(0)
-        activate(1)
-        activate(2)
-        activate(3)
-        activate(4)
-        second_layer(0, "pre_slot2")
-        second_layer(1, "pre_slot3")
+        for u in range(5):
+            activate(u)
+            if u < 2:
+                first_layer(u + BANKS)
+
+        second_layer(0, "sum2")
+        second_layer(1, "sum3")
         second_layer(2, "codes2")
-        gather_words(3, 1, "slot1")
+        gather_words(3, 1, "pos1")
         first_layer(6)
         first_layer(7)
-        hand_out(0, False)
-        hand_out(1, False)
-        hand_out(2, False)
+        for u in range(3):
+            hand_out(u, nc.scalar.copy)
+
         activate(5)
         second_layer(3, "codes3")
         second_layer(4, "codes4")
         activate(6)
         activate(7)
+
         second_layer(5, "codes5")
         second_layer(6, "codes6")
-        hand_out(3, True)
+        hand_out(3, nc.vector.tensor_copy)
         second_layer(7, "codes7")
-        hand_out(4, False)
-        hand_out(5, False)
-        hand_out(6, True)
-        hand_out(7, True)
+        hand_out(4, nc.scalar.copy)
+        hand_out(5, nc.scalar.copy)
+        hand_out(6, nc.vector.tensor_copy)
+        hand_out_last()

@@ -22,6 +22,8 @@ QUADRANT = 32
 LIST_ROWS = 16
 UNIT = 128
 CHUNK = 256
+W1_SPLIT = 304
+W1_PIECES = ((0, W1_SPLIT), (W1_SPLIT, H))
 UNITS = S // UNIT
 BANKS = 4
 HALVED_FROM = UNITS - 2
@@ -42,8 +44,8 @@ def tile_picked_embpos_gelu_p_kernel(tc, x_words, x_scales, w1, w2_words, w2_sca
                 nc.sync.dma_start(plane[r:P:QUADRANT, :].bitcast(I32), rows[r::PACK, :].bitcast(I32))
 
         w1_rows = w1.rearrange("(p j) c -> p j c", j=PACK)
-        w1_raw = [held.tile([P, PACK, H // 2], F32, name="w1_raw%d" % half) for half in range(2)]
-        nc.sync.dma_start(w1_raw[0][:], w1_rows[:, :, : H // 2])
+        w1_raw = [held.tile([P, PACK, hi - lo], F32, name="w1_raw%d" % lo) for lo, hi in W1_PIECES]
+        nc.sync.dma_start(w1_raw[0][:], w1_rows[:, :, :W1_SPLIT])
 
         offsets = held.tile([P, S // LIST_ROWS], U16, name="offsets")
         nc.sync.dma_start(offsets[:], offs)
@@ -57,7 +59,7 @@ def tile_picked_embpos_gelu_p_kernel(tc, x_words, x_scales, w1, w2_words, w2_sca
         nc.vector.memset(zero_in[:], 0.0)
         nc.scalar.activation(zero_bias[:], zero_in[:], GELU)
 
-        nc.sync.dma_start(w1_raw[1][:], w1_rows[:, :, H // 2 :])
+        nc.sync.dma_start(w1_raw[1][:], w1_rows[:, :, W1_SPLIT:])
 
         word_table = held.tile([P, T], U32, name="word_table", align_bytes=64)
         nc.sync.dma_start(word_table[:].bitcast(I32), x_words[0].rearrange("p n r -> p (n r)").bitcast(I32))
@@ -83,10 +85,10 @@ def tile_picked_embpos_gelu_p_kernel(tc, x_words, x_scales, w1, w2_words, w2_sca
         nc.vector.tensor_copy(x_plane[:], scale_table[:].indirect(offsets[:]))
 
         w1_grouped = held.tile([P, PACK, P, PACK], BF16, name="w1_grouped", align_bytes=64)
-        for half in range(2):
+        for piece, (lo, hi) in enumerate(W1_PIECES):
             nc.scalar.copy(
-                w1_grouped[:, :, half * P // 2 : (half + 1) * P // 2, :].rearrange("p t m j -> p m j t"),
-                w1_raw[half][:].rearrange("p j (m t) -> p m j t", t=PACK),
+                w1_grouped[:, :, lo // PACK : hi // PACK, :].rearrange("p t m j -> p m j t"),
+                w1_raw[piece][:].rearrange("p j (m t) -> p m j t", t=PACK),
             )
         w1_codes = held.tile([P, H], U32, name="w1_codes", align_bytes=64)
         w1_plane = held.tile([P, H], U8, name="w1_plane", align_bytes=64)

@@ -26,9 +26,7 @@ W1_SPLIT = 304
 W1_PIECES = ((0, W1_SPLIT), (W1_SPLIT, H))
 UNITS = S // UNIT
 BANKS = 4
-HALVED_FROM = UNITS - 2
 STORE_GROUPS = ((0, 3), (3, 4), (4, 5), (5, 6), (6, 7), (7, 8))
-STAGE_BYTES = N // P * UNIT * 4
 
 
 def tile_picked_embpos_gelu_p_kernel(tc, x_words, x_scales, w1, w2_words, w2_scales, pos, offs, out):
@@ -134,19 +132,25 @@ def tile_picked_embpos_gelu_p_kernel(tc, x_words, x_scales, w1, w2_words, w2_sca
             )
 
         def activate(u):
-            width = UNIT // 2 if u >= HALVED_FROM else UNIT
-            for lo in range(0, UNIT, width):
-                add_and_gelu(u, lo, lo + width)
+            cuts = {UNITS - 2: (0, 64, UNIT), UNITS - 1: (0, 64, 96, UNIT)}.get(u, (0, UNIT))
+            for lo, hi in zip(cuts, cuts[1:]):
+                add_and_gelu(u, lo, hi)
 
         def result_bank(u, m):
-            if u == UNITS - 1 and m == 1:
-                return banks1[0][:, 0, :]
+            if u == UNITS - 1:
+                return banks1[m][:, 0, :]
             return banks2[u % BANKS][:, m, :]
 
         def second_layer(u, tag):
             h_codes = held.tile([P, UNIT], U32, name="h_codes%d" % u, tag=tag, align_bytes=64)
             h_plane = held.tile([P, UNIT], U8, name="h_plane%d" % u, align_bytes=64)
-            nc.vector.quantize_mx(out=h_codes[:].bitcast(FP8X4), scales=h_plane[:], in_=hidden[u][:].rearrange("p n t -> p (n t)"))
+            width = UNIT // 2 if u == UNITS - 1 else UNIT
+            for lo in range(0, UNIT, width):
+                nc.vector.quantize_mx(
+                    out=h_codes[:, lo : lo + width].bitcast(FP8X4),
+                    scales=h_plane[:, lo : lo + width],
+                    in_=hidden[u][:, lo : lo + width, :].rearrange("p n t -> p (n t)"),
+                )
             for m in range(N // P):
                 nc.tensor.matmul_mx(
                     out=result_bank(u, m),
@@ -160,8 +164,8 @@ def tile_picked_embpos_gelu_p_kernel(tc, x_words, x_scales, w1, w2_words, w2_sca
 
         def staging_tile(first, last):
             shape = [P, N // P, (last - first) * UNIT]
-            if first in (3, 4):
-                return late.tile(shape, F32, name="staged%d" % first, align_bytes=64, offset=(first - 3) * STAGE_BYTES)
+            if first == 4:
+                return late.tile(shape, F32, name="staged%d" % first, align_bytes=64, offset=0)
             tag = "sum%d" % (UNITS - 1) if first == UNITS - 2 else "stage%d" % first
             return held.tile(shape, F32, name="staged%d" % first, tag=tag, align_bytes=64)
 
@@ -204,12 +208,12 @@ def tile_picked_embpos_gelu_p_kernel(tc, x_words, x_scales, w1, w2_words, w2_sca
         activate(5)
         second_layer(3, "codes3")
         second_layer(4, "codes4")
+        hand_out(3, nc.scalar.copy)
         activate(6)
         activate(7)
 
         second_layer(5, "codes5")
         second_layer(6, "codes6")
-        hand_out(3, nc.vector.tensor_copy)
         second_layer(7, "codes7")
         hand_out(4, nc.scalar.copy)
         hand_out(5, nc.scalar.copy)

@@ -208,8 +208,11 @@ def tile_picked_embpos_gelu_p_kernel(tc, x_words, x_scales, w1, w2_words, w2_sca
         activate(5)
         second_layer(3, "codes3")
         second_layer(4, "codes4")
-        hand_out(3, nc.scalar.copy)
+        shared = staging_tile(3, 4)
+        nc.scalar.copy(shared[:, 0, :], result_bank(3, 0))
         activate(6)
+        nc.vector.tensor_copy(shared[:, 1, :], result_bank(3, 1))
+        nc.sync.dma_start(out_rows[:, :, 3 * UNIT : 4 * UNIT], shared[:])
         activate(7)
 
         second_layer(5, "codes5")

@@ -97,6 +97,7 @@ def tile_picked_embpos_gelu_p_kernel(tc, x_words, x_scales, w1, w2_words, w2_sca
         x_codes = {}
         banks1 = [psum1.tile([P, PACK, UNIT], F32, name="acc1_%d" % b) for b in range(BANKS)]
         banks2 = [psum2.tile([P, N // P, UNIT], F32, name="acc2_%d" % b) for b in range(BANKS)]
+        first_bank = [banks1[b] for b in (0, 1, 2, 3, 1, 3, 0, 2)]
         hidden = [held.tile([P, UNIT, PACK], BF16, name="h%d" % u, tag="hidden%d" % u, align_bytes=64) for u in range(UNITS)]
         sums = [held.tile([P, PACK, UNIT], F32, name="pre%d" % u, tag="sum%d" % u, align_bytes=64) for u in range(UNITS)]
 
@@ -111,7 +112,7 @@ def tile_picked_embpos_gelu_p_kernel(tc, x_words, x_scales, w1, w2_words, w2_sca
             cols = slice(within * UNIT, (within + 1) * UNIT)
             for t in range(PACK):
                 nc.tensor.matmul_mx(
-                    out=banks1[u % BANKS][:, t, :],
+                    out=first_bank[u][:, t, :],
                     lhsT=w1_codes[:, t * P : (t + 1) * P].bitcast(FP8X4),
                     lhsT_scale=w1_plane[:, t * P : (t + 1) * P],
                     rhs=x_codes[c][:, cols].bitcast(FP8X4),
@@ -123,7 +124,7 @@ def tile_picked_embpos_gelu_p_kernel(tc, x_words, x_scales, w1, w2_words, w2_sca
         def add_and_gelu(u, lo, hi):
             c, within = divmod(u, per_chunk)
             at = within * UNIT
-            nc.vector.tensor_tensor(sums[u][:, :, lo:hi], banks1[u % BANKS][:, :, lo:hi], pos_chunks[c][:, :, at + lo : at + hi], ADD)
+            nc.vector.tensor_tensor(sums[u][:, :, lo:hi], first_bank[u][:, :, lo:hi], pos_chunks[c][:, :, at + lo : at + hi], ADD)
             nc.scalar.activation(
                 hidden[u][:, lo:hi, :].rearrange("p (c i) t -> p c t i", i=4),
                 sums[u][:, :, lo:hi].rearrange("p t (c i) -> p c t i", i=4),
@@ -138,7 +139,7 @@ def tile_picked_embpos_gelu_p_kernel(tc, x_words, x_scales, w1, w2_words, w2_sca
 
         def result_bank(u, m):
             if u == UNITS - 1:
-                return banks1[m][:, 0, :]
+                return banks1[2 * m + 1][:, 0, :]
             return banks2[u % BANKS][:, m, :]
 
         def second_layer(u, tag):
@@ -193,8 +194,8 @@ def tile_picked_embpos_gelu_p_kernel(tc, x_words, x_scales, w1, w2_words, w2_sca
             first_layer(u)
         for u in range(5):
             activate(u)
-            if u < 2:
-                first_layer(u + BANKS)
+            if u in (1, 3):
+                first_layer(BANKS + u // 2)
 
         second_layer(0, "sum2")
         second_layer(1, "sum3")

@@ -34,6 +34,7 @@ def tile_picked_embpos_gelu_p_kernel(tc, x_words, x_scales, w1, w2_words, w2_sca
     with ExitStack() as ctx:
         held = ctx.enter_context(tc.tile_pool(name="held", bufs=1))
         late = ctx.enter_context(tc.tile_pool(name="late", bufs=1))
+        spent = ctx.enter_context(tc.tile_pool(name="spent", bufs=1))
         psum1 = ctx.enter_context(tc.psum_pool(name="psum1", bufs=1))
         psum2 = ctx.enter_context(tc.psum_pool(name="psum2", bufs=1))
 
@@ -99,7 +100,8 @@ def tile_picked_embpos_gelu_p_kernel(tc, x_words, x_scales, w1, w2_words, w2_sca
         banks2 = [psum2.tile([P, N // P, UNIT], F32, name="acc2_%d" % b) for b in range(BANKS)]
         first_bank = [banks1[b] for b in (0, 1, 2, 3, 1, 3, 0, 2)]
         hidden = [held.tile([P, UNIT, PACK], BF16, name="h%d" % u, tag="hidden%d" % u, align_bytes=64) for u in range(UNITS)]
-        sums = [held.tile([P, PACK, UNIT], F32, name="pre%d" % u, tag="sum%d" % u, align_bytes=64) for u in range(UNITS)]
+        sums = [held.tile([P, PACK, UNIT], F32, name="pre%d" % u, tag="sum%d" % u, align_bytes=64) for u in range(UNITS) if u != 2]
+        sums = sums[:2] + [spent.tile([P, PACK, UNIT], F32, name="pre2", align_bytes=64, offset=0)] + sums[2:]
 
         def gather_words(first, count, tag):
             codes = held.tile([P, count * CHUNK], U32, name="x_codes%d" % first, tag=tag, align_bytes=64)
@@ -143,7 +145,10 @@ def tile_picked_embpos_gelu_p_kernel(tc, x_words, x_scales, w1, w2_words, w2_sca
             return banks2[u % BANKS][:, m, :]
 
         def second_layer(u, tag):
-            h_codes = held.tile([P, UNIT], U32, name="h_codes%d" % u, tag=tag, align_bytes=64)
+            if tag is None:
+                h_codes = spent.tile([P, UNIT], U32, name="h_codes%d" % u, align_bytes=64, offset=4 * UNIT * u)
+            else:
+                h_codes = held.tile([P, UNIT], U32, name="h_codes%d" % u, tag=tag, align_bytes=64)
             h_plane = held.tile([P, UNIT], U8, name="h_plane%d" % u, align_bytes=64)
             width = UNIT // 2 if u == UNITS - 1 else UNIT
             for lo in range(0, UNIT, width):
@@ -197,8 +202,8 @@ def tile_picked_embpos_gelu_p_kernel(tc, x_words, x_scales, w1, w2_words, w2_sca
             if u in (1, 3):
                 first_layer(BANKS + u // 2)
 
-        second_layer(0, "sum2")
-        second_layer(1, "sum3")
+        second_layer(0, None)
+        second_layer(1, None)
         second_layer(2, "codes2")
         gather_words(3, 1, "pos1")
         first_layer(6)

from contextlib import ExitStack

import concourse.mybir as mybir

K, T, S, H, N = 512, 2048, 1024, 512, 256
FLOPS = 2 * K * H * S + 2 * H * N * S

F32 = mybir.dt.float32
BF16 = mybir.dt.bfloat16
I32 = mybir.dt.int32
U32 = mybir.dt.uint32
U16 = mybir.dt.uint16
U8 = mybir.dt.uint8
FP8X4 = mybir.dt.float8_e4m3fn_x4
FP4X4 = mybir.dt.float4_e2m1fn_x4
GELU = mybir.ActivationFunctionType.Gelu_apprx_tanh
ADD = mybir.AluOpType.add

P = 128
PACK = 4
QUADRANT = 32
LIST_ROWS = 16
UNIT = 128
CHUNK = 256
W1_SPLIT = 304
W1_PIECES = ((0, W1_SPLIT), (W1_SPLIT, H))
UNITS = S // UNIT
BANKS = 4
STORE_GROUPS = ((0, 3), (3, 4), (4, 5), (5, 6), (6, 7), (7, 8))


def tile_picked_embpos_gelu_p_kernel(tc, x_words, x_scales, w1, w2_words, w2_scales, pos, offs, out):
    nc = tc.nc
    with ExitStack() as ctx:
        held = ctx.enter_context(tc.tile_pool(name="held", bufs=1))
        late = ctx.enter_context(tc.tile_pool(name="late", bufs=1))
        spent = ctx.enter_context(tc.tile_pool(name="spent", bufs=1))
        psum1 = ctx.enter_context(tc.psum_pool(name="psum1", bufs=1))
        psum2 = ctx.enter_context(tc.psum_pool(name="psum2", bufs=1))

        def load_scale_rows(plane, rows):
            for r in range(PACK):
                nc.sync.dma_start(plane[r:P:QUADRANT, :].bitcast(I32), rows[r::PACK, :].bitcast(I32))

        w1_rows = w1.rearrange("(p j) c -> p j c", j=PACK)
        w1_raw = [held.tile([P, PACK, hi - lo], F32, name="w1_raw%d" % lo) for lo, hi in W1_PIECES]
        nc.sync.dma_start(w1_raw[0][:], w1_rows[:, :, :W1_SPLIT])

        offsets = held.tile([P, S // LIST_ROWS], U16, name="offsets")
        nc.sync.dma_start(offsets[:], offs)

        scale_table = held.tile([P, T], U8, name="scale_table", align_bytes=64)
        nc.vector.memset(scale_table[:].bitcast(I32), 0)
        load_scale_rows(scale_table, x_scales[0])

        zero_in = held.tile([P, 1], F32, name="zero_in")
        zero_bias = held.tile([P, 1], F32, name="zero_bias")
        nc.vector.memset(zero_in[:], 0.0)
        nc.scalar.activation(zero_bias[:], zero_in[:], GELU)

        nc.sync.dma_start(w1_raw[1][:], w1_rows[:, :, W1_SPLIT:])

        word_table = held.tile([P, T], U32, name="word_table", align_bytes=64)
        nc.sync.dma_start(word_table[:].bitcast(I32), x_words[0].rearrange("p n r -> p (n r)").bitcast(I32))

        w2_codes = held.tile([P, 2 * N], U8, name="w2_codes", align_bytes=64)
        w2_plane = held.tile([P, N], U8, name="w2_plane", align_bytes=64)
        nc.vector.memset(w2_plane[:].bitcast(I32), 0)

        pos_rows = pos.rearrange("(p t) n -> p t n", t=PACK)
        pos_chunks = []
        for c in range(S // CHUNK):
            if c == S // CHUNK - 1:
                pos_chunk = late.tile([P, PACK, CHUNK], F32, name="pos_chunk%d" % c, align_bytes=64, offset=0)
            else:
                pos_chunk = held.tile([P, PACK, CHUNK], F32, name="pos_chunk%d" % c, tag="pos%d" % c, align_bytes=64)
            nc.sync.dma_start(pos_chunk[:], pos_rows[:, :, c * CHUNK : (c + 1) * CHUNK])
            pos_chunks.append(pos_chunk)
            if c == 0:
                nc.sync.dma_start(w2_codes[:].bitcast(I32), w2_words[0].bitcast(I32))
                load_scale_rows(w2_plane, w2_scales[0])

        x_plane = held.tile([P, S], U8, name="x_plane", align_bytes=64)
        nc.vector.tensor_copy(x_plane[:], scale_table[:].indirect(offsets[:]))

        w1_grouped = held.tile([P, PACK, P, PACK], BF16, name="w1_grouped", align_bytes=64)
        for piece, (lo, hi) in enumerate(W1_PIECES):
            nc.scalar.copy(
                w1_grouped[:, :, lo // PACK : hi // PACK, :].rearrange("p t m j -> p m j t"),
                w1_raw[piece][:].rearrange("p j (m t) -> p m j t", t=PACK),
            )
        w1_codes = held.tile([P, H], U32, name="w1_codes", align_bytes=64)
        w1_plane = held.tile([P, H], U8, name="w1_plane", align_bytes=64)
        nc.vector.quantize_mx(out=w1_codes[:].bitcast(FP8X4), scales=w1_plane[:], in_=w1_grouped[:].rearrange("p t m j -> p (t m j)"))

        out_rows = out.rearrange("(m p) n -> p m n", p=P)
        per_chunk = CHUNK // UNIT
        x_codes = {}
        banks1 = [psum1.tile([P, PACK, UNIT], F32, name="acc1_%d" % b) for b in range(BANKS)]
        banks2 = [psum2.tile([P, N // P, UNIT], F32, name="acc2_%d" % b) for b in range(BANKS)]
        first_bank = [banks1[b] for b in (0, 1, 2, 3, 1, 3, 0, 2)]
        hidden = [held.tile([P, UNIT, PACK], BF16, name="h%d" % u, tag="hidden%d" % u, align_bytes=64) for u in range(UNITS)]
        sums = [held.tile([P, PACK, UNIT], F32, name="pre%d" % u, tag="sum%d" % u, align_bytes=64) for u in range(UNITS) if u != 2]
        sums = sums[:2] + [spent.tile([P, PACK, UNIT], F32, name="pre2", align_bytes=64, offset=0)] + sums[2:]

        def gather_words(first, count, tag):
            codes = held.tile([P, count * CHUNK], U32, name="x_codes%d" % first, tag=tag, align_bytes=64)
            nc.vector.tensor_copy(codes[:], word_table[:].indirect(offsets[:, first * CHUNK // LIST_ROWS : (first + count) * CHUNK // LIST_ROWS]))
            for i in range(count):
                x_codes.setdefault(first + i, codes[:, i * CHUNK : (i + 1) * CHUNK])

        def first_layer(u):
            c, within = divmod(u, per_chunk)
            cols = slice(within * UNIT, (within + 1) * UNIT)
            for t in range(PACK):
                nc.tensor.matmul_mx(
                    out=first_bank[u][:, t, :],
                    lhsT=w1_codes[:, t * P : (t + 1) * P].bitcast(FP8X4),
                    lhsT_scale=w1_plane[:, t * P : (t + 1) * P],
                    rhs=x_codes[c][:, cols].bitcast(FP8X4),
                    rhs_scale=x_plane[:, u * UNIT : (u + 1) * UNIT],
                    start=True,
                    stop=True,
                )

        def add_and_gelu(u, lo, hi):
            c, within = divmod(u, per_chunk)
            at = within * UNIT
            nc.vector.tensor_tensor(sums[u][:, :, lo:hi], first_bank[u][:, :, lo:hi], pos_chunks[c][:, :, at + lo : at + hi], ADD)
            nc.scalar.activation(
                hidden[u][:, lo:hi, :].rearrange("p (c i) t -> p c t i", i=4),
                sums[u][:, :, lo:hi].rearrange("p t (c i) -> p c t i", i=4),
                GELU,
                bias=zero_bias[:],
            )

        def activate(u):
            cuts = {UNITS - 2: (0, 64, UNIT), UNITS - 1: (0, 64, 96, UNIT)}.get(u, (0, UNIT))
            for lo, hi in zip(cuts, cuts[1:]):
                add_and_gelu(u, lo, hi)

        def result_bank(u, m):
            if u == UNITS - 1:
                return banks1[2 * m + 1][:, 0, :]
            return banks2[u % BANKS][:, m, :]

        def second_layer(u, tag):
            if tag is None:
                h_codes = spent.tile([P, UNIT], U32, name="h_codes%d" % u, align_bytes=64, offset=4 * UNIT * u)
            else:
                h_codes = held.tile([P, UNIT], U32, name="h_codes%d" % u, tag=tag, align_bytes=64)
            h_plane = held.tile([P, UNIT], U8, name="h_plane%d" % u, align_bytes=64)
            width = UNIT // 2 if u == UNITS - 1 else UNIT
            for lo in range(0, UNIT, width):
                nc.vector.quantize_mx(
                    out=h_codes[:, lo : lo + width].bitcast(FP8X4),
                    scales=h_plane[:, lo : lo + width],
                    in_=hidden[u][:, lo : lo + width, :].rearrange("p n t -> p (n t)"),
                )
            for m in range(N // P):
                nc.tensor.matmul_mx(
                    out=result_bank(u, m),
                    lhsT=w2_codes[:, 2 * P * m : 2 * P * (m + 1)].bitcast(FP4X4),
                    lhsT_scale=w2_plane[:, P * m : P * (m + 1)],
                    rhs=h_codes[:].bitcast(FP8X4),
                    rhs_scale=h_plane[:],
                    start=True,
                    stop=True,
                )

        def staging_tile(first, last):
            shape = [P, N // P, (last - first) * UNIT]
            if first == 4:
                return late.tile(shape, F32, name="staged%d" % first, align_bytes=64, offset=0)
            tag = "sum%d" % (UNITS - 1) if first == UNITS - 2 else "stage%d" % first
            return held.tile(shape, F32, name="staged%d" % first, tag=tag, align_bytes=64)

        staged = {}

        def hand_out(u, copy):
            first, last = [g for g in STORE_GROUPS if g[0] <= u < g[1]][0]
            if first not in staged:
                staged.setdefault(first, staging_tile(first, last))
            copy(staged[first][:, :, (u - first) * UNIT : (u - first + 1) * UNIT], banks2[u % BANKS][:])
            if u == last - 1:
                nc.sync.dma_start(out_rows[:, :, first * UNIT : last * UNIT], staged[first][:])

        def hand_out_last():
            u = UNITS - 1
            tile = staging_tile(u, UNITS)
            nc.scalar.copy(tile[:, 0, :], result_bank(u, 0))
            nc.vector.tensor_copy(tile[:, 1, :], result_bank(u, 1))
            for m in range(N // P):
                nc.sync.dma_start(out_rows[:, m, u * UNIT :], tile[:, m, :])

        gather_words(0, 1, "first_codes")
        gather_words(1, 2, "middle_codes")
        for u in range(BANKS):
            first_layer(u)
        for u in range(5):
            activate(u)
            if u in (1, 3):
                first_layer(BANKS + u // 2)

        second_layer(0, None)
        second_layer(1, None)
        second_layer(2, "codes2")
        gather_words(3, 1, "pos1")
        first_layer(6)
        first_layer(7)
        for u in range(3):
            hand_out(u, nc.scalar.copy)

        activate(5)
        second_layer(3, "codes3")
        second_layer(4, "codes4")
        shared = staging_tile(3, 4)
        nc.scalar.copy(shared[:, 0, :], result_bank(3, 0))
        activate(6)
        nc.vector.tensor_copy(shared[:, 1, :], result_bank(3, 1))
        nc.sync.dma_start(out_rows[:, :, 3 * UNIT : 4 * UNIT], shared[:])
        activate(7)

        second_layer(5, "codes5")
        second_layer(6, "codes6")
        second_layer(7, "codes7")
        hand_out(4, nc.scalar.copy)
        hand_out(5, nc.scalar.copy)
        hand_out(6, nc.vector.tensor_copy)
        hand_out_last()
